import numpy as np
import ml_dtypes


def mxq(x, axis, fmt="e4m3"):
    dtype, down = {"e4m3": (ml_dtypes.float8_e4m3fn, 7), "e5m2": (ml_dtypes.float8_e5m2, 14)}[fmt]
    v = np.moveaxis(np.asarray(x, np.float32).astype(ml_dtypes.bfloat16).astype(np.float64), axis, -1)
    blocks = v.reshape(v.shape[:-1] + (-1, 32))
    amax = np.abs(blocks).max(-1, keepdims=True)
    byte = np.maximum(np.where(amax > 0, np.frexp(amax)[1] - 1 + 127, 0) - down, 1)
    scale = np.exp2(byte - 127.0)
    codes = (blocks / scale).astype(np.float32).astype(dtype).astype(np.float64)
    return np.moveaxis((codes * scale).reshape(v.shape), -1, axis)


WIDE = False


def mx_kscale(k):
    if not WIDE:
        return np.ones(k)
    levels = np.array([10, -10, 5, -5, 0])
    if k % 512:
        return np.exp2(np.random.permutation(np.resize(levels, k // 32))).repeat(32)
    a = np.empty((k // 512, 16))
    for p in range(k // 512):
        a[p, :8] = np.random.permutation(np.resize(levels, 8))
        for g in range(8):
            far = levels[np.abs(levels - a[p, g]) >= 10]
            a[p, g + 8] = far[np.random.randint(len(far))]
    return np.exp2(a.ravel()).repeat(32)


def f64(x):
    return np.asarray(x).astype(np.float64)


def striped(idx):
    return np.tile(idx.reshape(-1, 16).T, (8, 1)).astype(np.uint16)


def unstriped(offs):
    return offs[:16].T.reshape(-1).astype(np.int64)


def striped8(idx):
    return np.concatenate([x.reshape(-1, 16).T for x in idx]).astype(np.uint16)


def runs(offs, k):
    lists = np.stack([offs[16 * r : 16 * r + 16].T.reshape(-1) for r in range(8)]).astype(np.int64)
    return lists[np.arange(k) % 512 // 64]


def pack_weight(w):
    k, n = w.shape
    w = f64(np.asarray(w, np.float32).astype(ml_dtypes.bfloat16)).reshape(k // 32, 32, n)
    amax = np.abs(w).max(1)
    byte = np.clip(np.where(amax > 0, np.frexp(amax)[1] - 1 + 127 - 7, 1), 1, 254)
    scaled = (w * np.exp2(127.0 - byte)[:, None, :]).reshape(k, n).astype(np.float32)
    words = np.ascontiguousarray(scaled.reshape(k // 512, 128, 4, n).transpose(0, 1, 3, 2)).astype(ml_dtypes.float8_e4m3fn).view(np.uint8)
    return words, np.ascontiguousarray(byte.astype(np.uint8).reshape(k // 512, 16, n))


def unpack_weight(words, scales):
    g, p, n, _ = words.shape
    vals = np.ascontiguousarray(words).view(ml_dtypes.float8_e4m3fn).astype(np.float64) * np.repeat(np.exp2(scales.astype(np.float64) - 127.0), 8, axis=1)[..., None]
    return vals.transpose(0, 1, 3, 2).reshape(g * 512, n)

def planes(y):
    n, m = y.shape
    v = y.astype(np.float32).astype(ml_dtypes.bfloat16).astype(np.float64).reshape(n // 32, 32, m)
    top = np.abs(v).max(1)
    byte = np.clip(np.where(top > 0, np.frexp(top)[1] - 1 + 127 - 7, 1), 1, 254)
    codes = (v * np.exp2(127.0 - byte)[:, None, :]).reshape(n, m).astype(np.float32).astype(ml_dtypes.float8_e4m3fn).view(np.uint8)
    words = codes.reshape(n // 512, 128, 4, m).transpose(0, 1, 3, 2)
    return np.ascontiguousarray(words), np.ascontiguousarray(byte.astype(np.uint8).reshape(n // 512, 16, m))


K, T, S, N, W = 512, 2048, 256, 512, 128


def setup_inputs():
    n = np.random.standard_normal
    s = mx_kscale(K)[:, None]
    packed_xT = pack_weight(n((K, T)) * s)
    perm = np.random.permutation(S)
    return {
        "x_words": packed_xT[0],
        "x_scales": packed_xT[1],
        "w1": (n((K, N)) / np.sqrt(2 * K) / s).astype(np.float32),
        "w2": (n((K, N)) / np.sqrt(2 * K) / s).astype(np.float32),
        "offs": striped(np.random.permutation(T)[:S]),
        "hz": striped8(np.random.randint(0, T, (8, S))),
        "n1": striped(perm[:W]),
        "n2": striped(perm[W:]),
    }


def reference(x_words, x_scales, w1, w2, offs, hz, n1, n2):
    xq = unpack_weight(x_words, x_scales)[:, unstriped(offs)]
    x_hz = unpack_weight(x_words, x_scales)[np.arange(K)[:, None], runs(hz, K)]
    h = mxq(f64(w1), 0, "e4m3").T @ xq + mxq(f64(w2), 0, "e4m3").T @ x_hz
    pb = h[:, unstriped(n2)]
    pa = h[:, unstriped(n1)]
    rb = pb - (0.5 * pa)
    ra = np.sqrt((pa) ** 2 + (pb) ** 2 + 0.25)
    ds = np.zeros((N, S))
    ds[:, unstriped(n1)] = ra
    out = ds.copy()
    out[:, unstriped(n2)] = rb
    return (out,) + planes(out)

@@ -1,0 +1,192 @@
+from contextlib import ExitStack
+
+import concourse.mybir as mybir
+
+K, T, S, N, W = 512, 2048, 256, 512, 128
+FLOPS = 2 * 2 * K * N * S
+
+F32 = mybir.dt.float32
+BF16 = mybir.dt.bfloat16
+I32 = mybir.dt.int32
+U32 = mybir.dt.uint32
+U16 = mybir.dt.uint16
+U8 = mybir.dt.uint8
+FP8X4 = mybir.dt.float8_e4m3fn_x4
+ACT = mybir.ActivationFunctionType
+ALU = mybir.AluOpType
+
+P = 128
+PACK = 4
+HALF = 64
+
+
+def tile_picked_othpolar_none_po_kernel(
+    tc, x_words, x_scales, w1, w2, offs, hz, n1, n2, out_0, out_1, out_2
+):
+    nc = tc.nc
+    with ExitStack() as ctx:
+        sb = ctx.enter_context(tc.tile_pool(name="sb", bufs=1))
+        ps = ctx.enter_context(tc.psum_pool(name="ps", bufs=1))
+
+        hz_t = sb.tile([P, S // 16], U16, name="hz_t")
+        offs_t = sb.tile([P, S // 16], U16, name="offs_t")
+        n1_t = sb.tile([P, W // 16], U16, name="n1_t")
+        n2_t = sb.tile([P, W // 16], U16, name="n2_t")
+        xw = sb.tile([P, T], U32, name="xw")
+        reuse = ctx.enter_context(tc.tile_pool(name="reuse", bufs=1))
+        xs = reuse.tile([P, T], U8, name="xs", offset=3072)
+        raw = [[sb.tile([P, PACK, N // 2], F32, name="raw%d0" % a), None] for a in range(2)]
+
+        xs32 = xs[:].bitcast(I32)
+        nc.vector.memset(xs32[:, 0:320], 0)
+        nc.gpsimd.memset(xs32[:, 320:512], 0)
+        nc.sync.dma_start(hz_t[:], hz)
+        nc.sync.dma_start(offs_t[:], offs)
+        nc.sync.dma_start(n1_t[:], n1)
+        nc.sync.dma_start(n2_t[:], n2)
+        nc.sync.dma_start(out=xs32[0:P:8, :], in_=x_scales[0].bitcast(I32))
+        nc.sync.dma_start(out=xw[:].bitcast(I32), in_=x_words[0].rearrange("p c r -> p (c r)").bitcast(I32))
+        w_rows = [w.rearrange("(p j) c -> p j c", j=PACK) for w in (w1, w2)]
+        for a in range(2):
+            nc.sync.dma_start(out=raw[a][0][:], in_=w_rows[a][:, :, 0 : N // 2])
+
+        picked = sb.tile([P, 2, S], U8, name="picked", align_bytes=64)
+        x_sc = sb.tile([P, 2, S], U8, name="x_sc", align_bytes=64)
+        nc.gpsimd.memset(x_sc[:].bitcast(I32), 0)
+        nc.vector.tensor_copy(picked[:, 0, :], xs[:].indirect(offs_t[:]))
+        nc.vector.tensor_copy(picked[:, 1, :], xs[:].indirect(hz_t[:]))
+        for r in range(4):
+            nc.sync.dma_start(out=x_sc[:].bitcast(I32)[r:P:32, :, :], in_=picked[:].bitcast(I32)[8 * r : P : 32, :, :])
+        for a in range(2):
+            raw[a][1] = reuse.tile([P, PACK, N // 2], F32, name="raw%d1" % a, offset=4096 * a)
+            nc.sync.dma_start(out=raw[a][1][:], in_=w_rows[a][:, :, N // 2 : N])
+        x_cd = [sb.tile([P, S], U32, name="x_cd%d" % a, align_bytes=64) for a in range(2)]
+        nc.vector.tensor_copy(x_cd[0][:], xw[:].indirect(offs_t[:]))
+        nc.vector.tensor_copy(x_cd[1][:], xw[:].indirect(hz_t[:]))
+
+        wb01 = [[sb.tile([P, 2, HALF, PACK], BF16, name="wb01_%d%d" % (a, h), align_bytes=64) for h in range(2)] for a in range(2)]
+        wb23 = [sb.tile([P, 2, 2, HALF, PACK], BF16, name="wb23_%d" % a, align_bytes=64) for a in range(2)]
+        w_cd01 = [[sb.tile([P, P], U32, name="w_cd01_%d%d" % (a, h), align_bytes=64) for h in range(2)] for a in range(2)]
+        w_sc01 = [[sb.tile([P, P], U8, name="w_sc01_%d%d" % (a, h), align_bytes=64) for h in range(2)] for a in range(2)]
+        w_cd23 = [sb.tile([P, 2 * P], U32, name="w_cd23_%d" % a, align_bytes=64) for a in range(2)]
+        w_sc23 = [sb.tile([P, 2 * P], U8, name="w_sc23_%d" % a, align_bytes=64) for a in range(2)]
+
+        def raw_pair(a, h, r0):
+            return raw[a][h][:].rearrange("p j (i r) -> p i j r", r=PACK)[:, :, :, r0 : r0 + 2]
+
+        def round01(a, h):
+            nc.vector.tensor_copy(out=wb01[a][h][:].rearrange("p e i j -> p i j e"), in_=raw_pair(a, h, 0))
+
+        def quant01(a, h):
+            nc.vector.quantize_mx(
+                out=w_cd01[a][h][:].bitcast(FP8X4), scales=w_sc01[a][h][:], in_=wb01[a][h][:].rearrange("p e i j -> p (e i j)")
+            )
+
+        def round23_out(a, h):
+            return wb23[a][:, :, h, :, :].rearrange("p e i j -> p i j e")
+
+        def quant23(a):
+            nc.vector.quantize_mx(
+                out=w_cd23[a][:].bitcast(FP8X4), scales=w_sc23[a][:], in_=wb23[a][:].rearrange("p e h i j -> p (e h i j)")
+            )
+
+        acc = [ps.tile([P, S], F32, name="acc%d" % t) for t in range(4)]
+        h_sb = [sb.tile([P, S], F32, name="h_sb%d" % t) for t in range(4)]
+        pp = [sb.tile([P, 2, W], F32, name="pp%d" % t) for t in range(4)]
+        sq = [sb.tile([P, 2, W], F32, name="sq%d" % t) for t in range(4)]
+        rb = [sb.tile([P, W], F32, name="rb%d" % t) for t in range(4)]
+        ss = [sb.tile([P, W], F32, name="ss%d" % t) for t in range(4)]
+        ra = [sb.tile([P, W], F32, name="ra%d" % t) for t in range(4)]
+        y = [sb.tile([P, S], F32, name="y%d" % t) for t in range(4)]
+
+        def product(t, a):
+            if t < 2:
+                cd, sc = w_cd01[a][t][:], w_sc01[a][t][:]
+            else:
+                cols = slice((t - 2) * P, (t - 1) * P)
+                cd, sc = w_cd23[a][:, cols], w_sc23[a][:, cols]
+            nc.tensor.matmul_mx(
+                out=acc[t][:], lhsT=cd.bitcast(FP8X4), lhsT_scale=sc,
+                rhs=x_cd[a][:].bitcast(FP8X4), rhs_scale=x_sc[:, a, :], start=(a == 0), stop=(a == 1),
+            )
+
+        def fetch(t):
+            nc.scalar.activation(out=pp[t][:, 0, :], in_=h_sb[t][:].indirect(n1_t[:]), func=ACT.Copy)
+            nc.scalar.activation(out=pp[t][:, 1, :], in_=h_sb[t][:].indirect(n2_t[:]), func=ACT.Copy)
+
+        def combine(t):
+            nc.vector.scalar_tensor_tensor(
+                out=rb[t][:], in0=pp[t][:, 0, :], scalar=-0.5, in1=pp[t][:, 1, :], op0=ALU.mult, op1=ALU.add
+            )
+            nc.vector.tensor_tensor(out=sq[t][:], in0=pp[t][:], in1=pp[t][:], op=ALU.mult)
+            nc.vector.scalar_tensor_tensor(
+                out=ss[t][:], in0=sq[t][:, 0, :], scalar=0.25, in1=sq[t][:, 1, :], op0=ALU.add, op1=ALU.add
+            )
+
+        def put_rb(t):
+            nc.scalar.activation(out=y[t][:].indirect(n2_t[:]), in_=rb[t][:], func=ACT.Copy)
+
+        def root(t):
+            nc.scalar.activation(out=ra[t][:], in_=ss[t][:], func=ACT.Sqrt)
+
+        def put_ra(t):
+            nc.scalar.activation(out=y[t][:].indirect(n1_t[:]), in_=ra[t][:], func=ACT.Copy)
+
+        for a in range(2):
+            round01(a, 0)
+            nc.scalar.activation(out=round23_out(a, 0), in_=raw_pair(a, 0, 2), func=ACT.Copy)
+            quant01(a, 0)
+            product(0, a)
+        nc.scalar.copy(out=h_sb[0][:], in_=acc[0][:])
+        fetch(0)
+        round01(0, 1)
+        quant01(0, 1)
+        product(1, 0)
+        combine(0)
+        put_rb(0)
+        root(0)
+        round01(1, 1)
+        quant01(1, 1)
+        product(1, 1)
+        nc.vector.tensor_copy(out=h_sb[1][:], in_=acc[1][:])
+        for a in range(2):
+            nc.vector.tensor_copy(out=round23_out(a, 1), in_=raw_pair(a, 1, 2))
+        for a in range(2):
+            quant23(a)
+        for t in (2, 3):
+            for a in range(2):
+                product(t, a)
+
+        stage = sb.tile([P, 2, S], F32, name="stage")
+        yb = sb.tile([P, S, PACK], BF16, name="yb", align_bytes=64)
+        out_rows = out_0.rearrange("(p r) c -> p r c", r=PACK)
+
+        def finish(t):
+            if t < 2:
+                for e in range(2):
+                    nc.sync.dma_start(out=stage[t * HALF : (t + 1) * HALF, e, :], in_=y[t][e * HALF : (e + 1) * HALF, :])
+            else:
+                nc.sync.dma_start(out=out_rows[:, t, :], in_=y[t][:])
+                nc.vector.tensor_copy(out=yb[:, :, t], in_=y[t][:])
+
+        for t in range(1, 4):
+            fetch(t)
+            put_ra(t - 1)
+            combine(t)
+            if t < 3:
+                nc.vector.tensor_copy(out=h_sb[t + 1][:], in_=acc[t + 1][:])
+            finish(t - 1)
+            put_rb(t)
+            root(t)
+        nc.sync.dma_start(out=out_rows[:, 0:2, :], in_=stage[:])
+        nc.vector.tensor_copy(out=yb[:, :, 0:2], in_=stage[:].rearrange("p e c -> p c e"))
+        put_ra(3)
+        finish(3)
+
+        y_cd = sb.tile([P, S], U32, name="y_cd", align_bytes=64)
+        y_sc = sb.tile([P, S], U8, name="y_sc", align_bytes=64)
+        nc.vector.quantize_mx(out=y_cd[:].bitcast(FP8X4), scales=y_sc[:], in_=yb[:].rearrange("p c r -> p (c r)"))
+        nc.sync.dma_start(out=out_1[0].rearrange("p c r -> p (c r)").bitcast(I32), in_=y_cd[:].bitcast(I32))
+        for q in range(4):
+            eng = nc.scalar if q < 2 else nc.sync
+            eng.dma_start(out=out_2[0].bitcast(I32)[4 * q : 4 * q + 4, :], in_=y_sc[:].bitcast(I32)[32 * q : 32 * q + 4, :])

@@ -37,6 +37,10 @@ def tile_picked_othpolar_none_po_kernel(
         xs = reuse.tile([P, T], U8, name="xs", offset=3072)
         raw = [[sb.tile([P, PACK, N // 2], F32, name="raw%d0" % a), None] for a in range(2)]
 
+        warm = sb.tile([P, 2], F32, name="warm")
+        nc.gpsimd.memset(warm[:, 0:1], 1.0)
+        nc.scalar.activation(out=warm[:, 1:2], in_=warm[:, 0:1], func=ACT.Sqrt)
+
         xs32 = xs[:].bitcast(I32)
         nc.vector.memset(xs32[:, 0:320], 0)
         nc.gpsimd.memset(xs32[:, 320:512], 0)

@@ -44,15 +44,16 @@ def tile_picked_othpolar_none_po_kernel(
         xs32 = xs[:].bitcast(I32)
         nc.vector.memset(xs32[:, 0:320], 0)
         nc.gpsimd.memset(xs32[:, 320:512], 0)
+        w_rows = [w.rearrange("(p j) c -> p j c", j=PACK) for w in (w1, w2)]
+        nc.sync.dma_start(out=raw[0][0][:, 0:2, :], in_=w_rows[0][:, 0:2, 0 : N // 2])
         nc.sync.dma_start(hz_t[:], hz)
         nc.sync.dma_start(offs_t[:], offs)
+        nc.sync.dma_start(out=xs32[0:P:8, :], in_=x_scales[0].bitcast(I32))
+        nc.sync.dma_start(out=raw[0][0][:, 2:4, :], in_=w_rows[0][:, 2:4, 0 : N // 2])
         nc.sync.dma_start(n1_t[:], n1)
         nc.sync.dma_start(n2_t[:], n2)
-        nc.sync.dma_start(out=xs32[0:P:8, :], in_=x_scales[0].bitcast(I32))
         nc.sync.dma_start(out=xw[:].bitcast(I32), in_=x_words[0].rearrange("p c r -> p (c r)").bitcast(I32))
-        w_rows = [w.rearrange("(p j) c -> p j c", j=PACK) for w in (w1, w2)]
-        for a in range(2):
-            nc.sync.dma_start(out=raw[a][0][:], in_=w_rows[a][:, :, 0 : N // 2])
+        nc.sync.dma_start(out=raw[1][0][:], in_=w_rows[1][:, :, 0 : N // 2])
 
         picked = sb.tile([P, 2, S], U8, name="picked", align_bytes=64)
         x_sc = sb.tile([P, 2, S], U8, name="x_sc", align_bytes=64)
@@ -95,13 +96,17 @@ def tile_picked_othpolar_none_po_kernel(
             )
 
         acc = [ps.tile([P, S], F32, name="acc%d" % t) for t in range(4)]
-        h_sb = [sb.tile([P, S], F32, name="h_sb%d" % t) for t in range(4)]
-        pp = [sb.tile([P, 2, W], F32, name="pp%d" % t) for t in range(4)]
-        sq = [sb.tile([P, 2, W], F32, name="sq%d" % t) for t in range(4)]
-        rb = [sb.tile([P, W], F32, name="rb%d" % t) for t in range(4)]
+        h_sb = [sb.tile([P, S], F32, name="h_sb%d" % t) for t in range(3)]
+        h_sb.append(reuse.tile([P, S], F32, name="h_sb3", offset=9216))
+        pp = [sb.tile([P, 2, W], F32, name="pp%d" % t) for t in range(3)]
+        sq = [None] + [sb.tile([P, 2, W], F32, name="sq%d" % t) for t in range(1, 4)]
+        rb = [None, None, None, sb.tile([P, W], F32, name="rb3")]
         ss = [sb.tile([P, W], F32, name="ss%d" % t) for t in range(4)]
-        ra = [sb.tile([P, W], F32, name="ra%d" % t) for t in range(4)]
-        y = [sb.tile([P, S], F32, name="y%d" % t) for t in range(4)]
+        ra = [sb.tile([P, W], F32, name="ra%d" % t) for t in range(3)]
+        y = [
+            reuse.tile([P, S], F32, name="y1", offset=10240) if t == 1 else sb.tile([P, S], F32, name="y%d" % t)
+            for t in range(4)
+        ]
 
         def product(t, a):
             if t < 2:
@@ -118,11 +123,15 @@ def tile_picked_othpolar_none_po_kernel(
             nc.scalar.activation(out=pp[t][:, 0, :], in_=h_sb[t][:].indirect(n1_t[:]), func=ACT.Copy)
             nc.scalar.activation(out=pp[t][:, 1, :], in_=h_sb[t][:].indirect(n2_t[:]), func=ACT.Copy)
 
-        def combine(t):
+        def differ(t):
             nc.vector.scalar_tensor_tensor(
                 out=rb[t][:], in0=pp[t][:, 0, :], scalar=-0.5, in1=pp[t][:, 1, :], op0=ALU.mult, op1=ALU.add
             )
+
+        def square(t):
             nc.vector.tensor_tensor(out=sq[t][:], in0=pp[t][:], in1=pp[t][:], op=ALU.mult)
+
+        def add_squares(t):
             nc.vector.scalar_tensor_tensor(
                 out=ss[t][:], in0=sq[t][:, 0, :], scalar=0.25, in1=sq[t][:, 1, :], op0=ALU.add, op1=ALU.add
             )
@@ -143,23 +152,25 @@ def tile_picked_othpolar_none_po_kernel(
             product(0, a)
         nc.scalar.copy(out=h_sb[0][:], in_=acc[0][:])
         fetch(0)
-        round01(0, 1)
-        quant01(0, 1)
-        product(1, 0)
-        combine(0)
-        put_rb(0)
-        root(0)
-        round01(1, 1)
-        quant01(1, 1)
-        product(1, 1)
-        nc.vector.tensor_copy(out=h_sb[1][:], in_=acc[1][:])
         for a in range(2):
+            round01(a, 1)
             nc.vector.tensor_copy(out=round23_out(a, 1), in_=raw_pair(a, 1, 2))
-        for a in range(2):
-            quant23(a)
-        for t in (2, 3):
-            for a in range(2):
-                product(t, a)
+            if a == 0:
+                quant01(a, 1)
+                quant23(a)
+                for t in range(1, 4):
+                    product(t, a)
+        rb[0] = reuse.tile([P, W], F32, name="rb0", offset=4096)
+        sq[0] = reuse.tile([P, 2, W], F32, name="sq0", offset=5120)
+        differ(0)
+        put_rb(0)
+        quant01(1, 1)
+        square(0)
+        quant23(1)
+        add_squares(0)
+        root(0)
+        for t in range(1, 4):
+            product(t, 1)
 
         stage = sb.tile([P, 2, S], F32, name="stage")
         yb = sb.tile([P, S, PACK], BF16, name="yb", align_bytes=64)
@@ -171,17 +182,37 @@ def tile_picked_othpolar_none_po_kernel(
                     nc.sync.dma_start(out=stage[t * HALF : (t + 1) * HALF, e, :], in_=y[t][e * HALF : (e + 1) * HALF, :])
             else:
                 nc.sync.dma_start(out=out_rows[:, t, :], in_=y[t][:])
-                nc.vector.tensor_copy(out=yb[:, :, t], in_=y[t][:])
 
         for t in range(1, 4):
-            fetch(t)
-            put_ra(t - 1)
-            combine(t)
-            if t < 3:
-                nc.vector.tensor_copy(out=h_sb[t + 1][:], in_=acc[t + 1][:])
-            finish(t - 1)
-            put_rb(t)
-            root(t)
+            nc.vector.tensor_copy(out=h_sb[t][:], in_=acc[t][:])
+        fetch(1)
+        put_ra(0)
+        finish(0)
+        fetch(2)
+        rb[1] = reuse.tile([P, W], F32, name="rb1", offset=8192)
+        differ(1)
+        for t in (1, 2):
+            square(t)
+            add_squares(t)
+        put_rb(1)
+        root(1)
+        pp.append(reuse.tile([P, 2, W], F32, name="pp3", offset=8192))
+        fetch(3)
+        put_ra(1)
+        finish(1)
+        root(2)
+        rb[2] = reuse.tile([P, W], F32, name="rb2", offset=9216)
+        differ(2)
+        differ(3)
+        square(3)
+        add_squares(3)
+        put_rb(2)
+        put_rb(3)
+        put_ra(2)
+        finish(2)
+        ra.append(reuse.tile([P, W], F32, name="ra3", offset=10240))
+        root(3)
+        nc.vector.tensor_copy(out=yb[:, :, 2], in_=y[2][:])
         nc.sync.dma_start(out=out_rows[:, 0:2, :], in_=stage[:])
         nc.vector.tensor_copy(out=yb[:, :, 0:2], in_=stage[:].rearrange("p e c -> p c e"))
         put_ra(3)
@@ -189,7 +220,14 @@ def tile_picked_othpolar_none_po_kernel(
 
         y_cd = sb.tile([P, S], U32, name="y_cd", align_bytes=64)
         y_sc = sb.tile([P, S], U8, name="y_sc", align_bytes=64)
-        nc.vector.quantize_mx(out=y_cd[:].bitcast(FP8X4), scales=y_sc[:], in_=yb[:].rearrange("p c r -> p (c r)"))
+        for c in range(2):
+            cols = slice(c * W, (c + 1) * W)
+            nc.vector.tensor_copy(out=yb[:, cols, 3], in_=y[3][:, cols])
+        for c in range(2):
+            cols = slice(c * W, (c + 1) * W)
+            nc.vector.quantize_mx(
+                out=y_cd[:, cols].bitcast(FP8X4), scales=y_sc[:, cols], in_=yb[:, cols, :].rearrange("p c r -> p (c r)")
+            )
         nc.sync.dma_start(out=out_1[0].rearrange("p c r -> p (c r)").bitcast(I32), in_=y_cd[:].bitcast(I32))
         for q in range(4):
             eng = nc.scalar if q < 2 else nc.sync

from contextlib import ExitStack

import concourse.mybir as mybir

K, T, S, N, W = 512, 2048, 256, 512, 128
FLOPS = 2 * 2 * K * N * S

F32 = mybir.dt.float32
BF16 = mybir.dt.bfloat16
I32 = mybir.dt.int32
U32 = mybir.dt.uint32
U16 = mybir.dt.uint16
U8 = mybir.dt.uint8
FP8X4 = mybir.dt.float8_e4m3fn_x4
ACT = mybir.ActivationFunctionType
ALU = mybir.AluOpType

P = 128
PACK = 4
HALF = 64


def tile_picked_othpolar_none_po_kernel(
    tc, x_words, x_scales, w1, w2, offs, hz, n1, n2, out_0, out_1, out_2
):
    nc = tc.nc
    with ExitStack() as ctx:
        sb = ctx.enter_context(tc.tile_pool(name="sb", bufs=1))
        ps = ctx.enter_context(tc.psum_pool(name="ps", bufs=1))

        hz_t = sb.tile([P, S // 16], U16, name="hz_t")
        offs_t = sb.tile([P, S // 16], U16, name="offs_t")
        n1_t = sb.tile([P, W // 16], U16, name="n1_t")
        n2_t = sb.tile([P, W // 16], U16, name="n2_t")
        xw = sb.tile([P, T], U32, name="xw")
        reuse = ctx.enter_context(tc.tile_pool(name="reuse", bufs=1))
        xs = reuse.tile([P, T], U8, name="xs", offset=3072)
        raw = [[sb.tile([P, PACK, N // 2], F32, name="raw%d0" % a), None] for a in range(2)]

        warm = sb.tile([P, 2], F32, name="warm")
        nc.gpsimd.memset(warm[:, 0:1], 1.0)
        nc.scalar.activation(out=warm[:, 1:2], in_=warm[:, 0:1], func=ACT.Sqrt)

        xs32 = xs[:].bitcast(I32)
        nc.vector.memset(xs32[:, 0:320], 0)
        nc.gpsimd.memset(xs32[:, 320:512], 0)
        w_rows = [w.rearrange("(p j) c -> p j c", j=PACK) for w in (w1, w2)]
        nc.sync.dma_start(out=raw[0][0][:, 0:2, :], in_=w_rows[0][:, 0:2, 0 : N // 2])
        nc.sync.dma_start(hz_t[:], hz)
        nc.sync.dma_start(offs_t[:], offs)
        nc.sync.dma_start(out=xs32[0:P:8, :], in_=x_scales[0].bitcast(I32))
        nc.sync.dma_start(out=raw[0][0][:, 2:4, :], in_=w_rows[0][:, 2:4, 0 : N // 2])
        nc.sync.dma_start(n1_t[:], n1)
        nc.sync.dma_start(n2_t[:], n2)
        nc.sync.dma_start(out=xw[:].bitcast(I32), in_=x_words[0].rearrange("p c r -> p (c r)").bitcast(I32))
        nc.sync.dma_start(out=raw[1][0][:], in_=w_rows[1][:, :, 0 : N // 2])

        picked = sb.tile([P, 2, S], U8, name="picked", align_bytes=64)
        x_sc = sb.tile([P, 2, S], U8, name="x_sc", align_bytes=64)
        nc.gpsimd.memset(x_sc[:].bitcast(I32), 0)
        nc.vector.tensor_copy(picked[:, 0, :], xs[:].indirect(offs_t[:]))
        nc.vector.tensor_copy(picked[:, 1, :], xs[:].indirect(hz_t[:]))
        for r in range(4):
            nc.sync.dma_start(out=x_sc[:].bitcast(I32)[r:P:32, :, :], in_=picked[:].bitcast(I32)[8 * r : P : 32, :, :])
        for a in range(2):
            raw[a][1] = reuse.tile([P, PACK, N // 2], F32, name="raw%d1" % a, offset=4096 * a)
            nc.sync.dma_start(out=raw[a][1][:], in_=w_rows[a][:, :, N // 2 : N])
        x_cd = [sb.tile([P, S], U32, name="x_cd%d" % a, align_bytes=64) for a in range(2)]
        nc.vector.tensor_copy(x_cd[0][:], xw[:].indirect(offs_t[:]))
        nc.vector.tensor_copy(x_cd[1][:], xw[:].indirect(hz_t[:]))

        wb01 = [[sb.tile([P, 2, HALF, PACK], BF16, name="wb01_%d%d" % (a, h), align_bytes=64) for h in range(2)] for a in range(2)]
        wb23 = [sb.tile([P, 2, 2, HALF, PACK], BF16, name="wb23_%d" % a, align_bytes=64) for a in range(2)]
        w_cd01 = [[sb.tile([P, P], U32, name="w_cd01_%d%d" % (a, h), align_bytes=64) for h in range(2)] for a in range(2)]
        w_sc01 = [[sb.tile([P, P], U8, name="w_sc01_%d%d" % (a, h), align_bytes=64) for h in range(2)] for a in range(2)]
        w_cd23 = [sb.tile([P, 2 * P], U32, name="w_cd23_%d" % a, align_bytes=64) for a in range(2)]
        w_sc23 = [sb.tile([P, 2 * P], U8, name="w_sc23_%d" % a, align_bytes=64) for a in range(2)]

        def raw_pair(a, h, r0):
            return raw[a][h][:].rearrange("p j (i r) -> p i j r", r=PACK)[:, :, :, r0 : r0 + 2]

        def round01(a, h):
            nc.vector.tensor_copy(out=wb01[a][h][:].rearrange("p e i j -> p i j e"), in_=raw_pair(a, h, 0))

        def quant01(a, h):
            nc.vector.quantize_mx(
                out=w_cd01[a][h][:].bitcast(FP8X4), scales=w_sc01[a][h][:], in_=wb01[a][h][:].rearrange("p e i j -> p (e i j)")
            )

        def round23_out(a, h):
            return wb23[a][:, :, h, :, :].rearrange("p e i j -> p i j e")

        def quant23(a):
            nc.vector.quantize_mx(
                out=w_cd23[a][:].bitcast(FP8X4), scales=w_sc23[a][:], in_=wb23[a][:].rearrange("p e h i j -> p (e h i j)")
            )

        acc = [ps.tile([P, S], F32, name="acc%d" % t) for t in range(4)]
        h_sb = [sb.tile([P, S], F32, name="h_sb%d" % t) for t in range(3)]
        h_sb.append(reuse.tile([P, S], F32, name="h_sb3", offset=9216))
        pp = [sb.tile([P, 2, W], F32, name="pp%d" % t) for t in range(3)]
        sq = [None] + [sb.tile([P, 2, W], F32, name="sq%d" % t) for t in range(1, 4)]
        rb = [None, None, None, sb.tile([P, W], F32, name="rb3")]
        ss = [sb.tile([P, W], F32, name="ss%d" % t) for t in range(4)]
        ra = [sb.tile([P, W], F32, name="ra%d" % t) for t in range(3)]
        y = [
            reuse.tile([P, S], F32, name="y1", offset=10240) if t == 1 else sb.tile([P, S], F32, name="y%d" % t)
            for t in range(4)
        ]

        def product(t, a):
            if t < 2:
                cd, sc = w_cd01[a][t][:], w_sc01[a][t][:]
            else:
                cols = slice((t - 2) * P, (t - 1) * P)
                cd, sc = w_cd23[a][:, cols], w_sc23[a][:, cols]
            nc.tensor.matmul_mx(
                out=acc[t][:], lhsT=cd.bitcast(FP8X4), lhsT_scale=sc,
                rhs=x_cd[a][:].bitcast(FP8X4), rhs_scale=x_sc[:, a, :], start=(a == 0), stop=(a == 1),
            )

        def fetch(t):
            nc.scalar.activation(out=pp[t][:, 0, :], in_=h_sb[t][:].indirect(n1_t[:]), func=ACT.Copy)
            nc.scalar.activation(out=pp[t][:, 1, :], in_=h_sb[t][:].indirect(n2_t[:]), func=ACT.Copy)

        def differ(t):
            nc.vector.scalar_tensor_tensor(
                out=rb[t][:], in0=pp[t][:, 0, :], scalar=-0.5, in1=pp[t][:, 1, :], op0=ALU.mult, op1=ALU.add
            )

        def square(t):
            nc.vector.tensor_tensor(out=sq[t][:], in0=pp[t][:], in1=pp[t][:], op=ALU.mult)

        def add_squares(t):
            nc.vector.scalar_tensor_tensor(
                out=ss[t][:], in0=sq[t][:, 0, :], scalar=0.25, in1=sq[t][:, 1, :], op0=ALU.add, op1=ALU.add
            )

        def put_rb(t):
            nc.scalar.activation(out=y[t][:].indirect(n2_t[:]), in_=rb[t][:], func=ACT.Copy)

        def root(t):
            nc.scalar.activation(out=ra[t][:], in_=ss[t][:], func=ACT.Sqrt)

        def put_ra(t):
            nc.scalar.activation(out=y[t][:].indirect(n1_t[:]), in_=ra[t][:], func=ACT.Copy)

        for a in range(2):
            round01(a, 0)
            nc.scalar.activation(out=round23_out(a, 0), in_=raw_pair(a, 0, 2), func=ACT.Copy)
            quant01(a, 0)
            product(0, a)
        nc.scalar.copy(out=h_sb[0][:], in_=acc[0][:])
        fetch(0)
        for a in range(2):
            round01(a, 1)
            nc.vector.tensor_copy(out=round23_out(a, 1), in_=raw_pair(a, 1, 2))
            if a == 0:
                quant01(a, 1)
                quant23(a)
                for t in range(1, 4):
                    product(t, a)
        rb[0] = reuse.tile([P, W], F32, name="rb0", offset=4096)
        sq[0] = reuse.tile([P, 2, W], F32, name="sq0", offset=5120)
        differ(0)
        put_rb(0)
        quant01(1, 1)
        square(0)
        quant23(1)
        add_squares(0)
        root(0)
        for t in range(1, 4):
            product(t, 1)

        stage = sb.tile([P, 2, S], F32, name="stage")
        yb = sb.tile([P, S, PACK], BF16, name="yb", align_bytes=64)
        out_rows = out_0.rearrange("(p r) c -> p r c", r=PACK)

        def finish(t):
            if t < 2:
                for e in range(2):
                    nc.sync.dma_start(out=stage[t * HALF : (t + 1) * HALF, e, :], in_=y[t][e * HALF : (e + 1) * HALF, :])
            else:
                nc.sync.dma_start(out=out_rows[:, t, :], in_=y[t][:])

        for t in range(1, 4):
            nc.vector.tensor_copy(out=h_sb[t][:], in_=acc[t][:])
        fetch(1)
        put_ra(0)
        finish(0)
        fetch(2)
        rb[1] = reuse.tile([P, W], F32, name="rb1", offset=8192)
        differ(1)
        for t in (1, 2):
            square(t)
            add_squares(t)
        put_rb(1)
        root(1)
        pp.append(reuse.tile([P, 2, W], F32, name="pp3", offset=8192))
        fetch(3)
        put_ra(1)
        finish(1)
        root(2)
        rb[2] = reuse.tile([P, W], F32, name="rb2", offset=9216)
        differ(2)
        differ(3)
        square(3)
        add_squares(3)
        put_rb(2)
        put_rb(3)
        put_ra(2)
        finish(2)
        ra.append(reuse.tile([P, W], F32, name="ra3", offset=10240))
        root(3)
        nc.vector.tensor_copy(out=yb[:, :, 2], in_=y[2][:])
        nc.sync.dma_start(out=out_rows[:, 0:2, :], in_=stage[:])
        nc.vector.tensor_copy(out=yb[:, :, 0:2], in_=stage[:].rearrange("p e c -> p c e"))
        put_ra(3)
        finish(3)

        y_cd = sb.tile([P, S], U32, name="y_cd", align_bytes=64)
        y_sc = sb.tile([P, S], U8, name="y_sc", align_bytes=64)
        for c in range(2):
            cols = slice(c * W, (c + 1) * W)
            nc.vector.tensor_copy(out=yb[:, cols, 3], in_=y[3][:, cols])
        for c in range(2):
            cols = slice(c * W, (c + 1) * W)
            nc.vector.quantize_mx(
                out=y_cd[:, cols].bitcast(FP8X4), scales=y_sc[:, cols], in_=yb[:, cols, :].rearrange("p c r -> p (c r)")
            )
        nc.sync.dma_start(out=out_1[0].rearrange("p c r -> p (c r)").bitcast(I32), in_=y_cd[:].bitcast(I32))
        for q in range(4):
            eng = nc.scalar if q < 2 else nc.sync
            eng.dma_start(out=out_2[0].bitcast(I32)[4 * q : 4 * q + 4, :], in_=y_sc[:].bitcast(I32)[32 * q : 32 * q + 4, :])
